import numpy as np, ml_dtypes
CORES = [6,7,14,15,22,23,30,31,38,39,46,47,54,55,62,63]
N = 16
WIDTHS = [4,8,1,4,2,4,4,16,8,4,8,1,4,8,8,0]
OFF = [0,4,12,13,17,19,23,27,43,51,55,63,64,68,76,84]
C = 84
def setup_inputs(rng):
    return {"x": rng.standard_normal((N, 128, C), dtype=np.float32).astype(ml_dtypes.bfloat16)}
def reference(x):
    s = x.sum(axis=0, dtype=np.float64).astype(x.dtype)
    YW = max(WIDTHS)
    y = np.full((N, 128, YW), np.nan, x.dtype)
    for r in range(N):
        y[r][:, :WIDTHS[r]] = s[:, OFF[r]:OFF[r] + WIDTHS[r]]
    return {"y": y}

@@ -1,0 +1,110 @@
+from concourse.bass import DstId, RemoteDMATransfer
+
+P = 7
+NCOL = 12
+G = 2
+NR = 16
+
+SCRATCH = {
+    "xs": ("dram", [P * 128, NCOL], "bfloat16"),
+    "land": ("dram", [NR * 128, NCOL], "bfloat16"),
+    "s": ("dram", [P * 128, NCOL], "bfloat16"),
+}
+SEMAPHORES = ["ld", "snt", "arr", "res", "st", "stg"]
+
+
+def helper_core(j, q):
+    if G == 1:
+        return 8 * j + 2
+    return 8 * (q + 2 * (j % 4)) + 4 + j // 4
+
+
+def served_chips(q):
+    return list(range(8)) if G == 1 else [q, q + 2, q + 4, q + 6]
+
+
+def blk(t, k):
+    return t[128 * k:128 * (k + 1), :]
+
+
+def segments(off, w, yw):
+    out = []
+    c = off
+    while c < off + w:
+        e = min(off + w, (c // NCOL + 1) * NCOL)
+        out.append([c, e, False])
+        c = e
+    for k, sg in enumerate(out):
+        if sg[1] - sg[0] == 1:
+            if k == len(out) - 1 and sg[0] % NCOL + 2 <= NCOL and sg[0] - off + 2 <= yw:
+                sg[1] += 1
+            else:
+                sg[2] = True
+    return out
+
+
+def dst_id(topo, c):
+    a = topo.addr(c)
+    return DstId(rid=a[0], pnc=a[1])
+
+
+def rank_program(g, core, T, topo):
+    widths = T.tables["WIDTHS"]
+    offs = T.tables["OFF"]
+    rank = T.rank_of(core)
+    eng2 = 8 // len(served_chips(0))
+
+    if rank is not None:
+        g.sync.dma_start(T.xs[:], T.x[:]).then_inc(T.sem.ld, 16)
+        g.wait_ge(T.sem.ld, 16)
+        trs = []
+        for j in range(P):
+            hs = [helper_core(j, q) for q in range(G)]
+            trs.append(RemoteDMATransfer(
+                dst_ids=[dst_id(topo, h) for h in hs], dma_engine_mask=1 << j, remote_sem=T.sem.arr,
+                srcs=[blk(T.xs, j)], dsts=[blk(T.land, rank) for h in hs], alu_op=0))
+        g.remote_dma_fused(trs, local_sem=T.sem.snt)
+        w = widths[rank]
+        if w > 0:
+            need = P * eng2
+            hw = [g.sync, g.scalar]
+            waited = [False, False]
+            nhw = 0
+            nsw = 0
+            for c, e, lone in segments(offs[rank], w, T.y.shape[1]):
+                src = T.s[c // NCOL::P, c % NCOL:c % NCOL + e - c]
+                dst = T.y[:, c - offs[rank]:e - offs[rank]]
+                if lone:
+                    g.wait_ge(T.sem.res, need)
+                    g.dma_start(dst, src, allow_slow_non_contiguous=True).then_inc(T.sem.stg, 16)
+                    nsw += 1
+                else:
+                    k = nhw % 2
+                    if not waited[k]:
+                        hw[k].wait_ge(T.sem.res, need)
+                        waited[k] = True
+                    hw[k].dma_start(dst, src).then_inc(T.sem.st, 16)
+                    nhw += 1
+            g.wait_ge(T.sem.res, need)
+            if nhw:
+                g.wait_ge(T.sem.st, 16 * nhw)
+            if nsw:
+                g.wait_ge(T.sem.stg, 16 * nsw)
+        g.wait_ge(T.sem.snt, P)
+        return
+
+    for j in range(P):
+        for q in range(G):
+            if helper_core(j, q) != core:
+                continue
+            g.wait_ge(T.sem.arr, NR)
+            srcs = [blk(T.land, i) for i in range(NR)]
+            trs = []
+            for t, ch in enumerate(served_chips(q)):
+                ds = [c for c in T.cores if topo.chip(c) == ch and widths[T.rank_of(c)] > 0]
+                trs.append(RemoteDMATransfer(
+                    dst_ids=[dst_id(topo, c) for c in ds],
+                    dma_engine_mask=((1 << eng2) - 1) << (eng2 * t), remote_sem=T.sem.res,
+                    srcs=srcs, dsts=[blk(T.s, j) for c in ds], alu_op=1))
+            g.remote_dma_fused(trs, local_sem=T.sem.snt)
+            g.wait_ge(T.sem.snt, eng2 * len(trs))

@@ -2,25 +2,29 @@ from concourse.bass import DstId, RemoteDMATransfer
 
 P = 7
 NCOL = 12
-G = 2
+GROUPS = [[0, 2, 4, 6], [1, 3, 5, 7]]
+HCORES = [4, 5]
+SPW = 4
+G = len(GROUPS)
 NR = 16
 
 SCRATCH = {
     "xs": ("dram", [P * 128, NCOL], "bfloat16"),
     "land": ("dram", [NR * 128, NCOL], "bfloat16"),
     "s": ("dram", [P * 128, NCOL], "bfloat16"),
+    "xb": ("dram", [128, SPW], "bfloat16"),
+    "lb": ("dram", [NR * 128, SPW], "bfloat16"),
+    "sb": ("dram", [128, SPW], "bfloat16"),
 }
-SEMAPHORES = ["ld", "snt", "arr", "res", "st", "stg"]
+SEMAPHORES = ["ld", "ld2", "snt", "arr", "res", "st"]
 
 
-def helper_core(j, q):
-    if G == 1:
-        return 8 * j + 2
-    return 8 * (q + 2 * (j % 4)) + 4 + j // 4
-
-
-def served_chips(q):
-    return list(range(8)) if G == 1 else [q, q + 2, q + 4, q + 6]
+def helper_core(j, q, sp_chip):
+    chips = GROUPS[q]
+    if j < len(chips):
+        return 8 * chips[j] + HCORES[0]
+    rest = [ch for ch in chips if ch != sp_chip]
+    return 8 * rest[j - len(chips)] + HCORES[1]
 
 
 def blk(t, k):
@@ -51,60 +55,66 @@ def dst_id(topo, c):
 def rank_program(g, core, T, topo):
     widths = T.tables["WIDTHS"]
     offs = T.tables["OFF"]
+    yw = 16
     rank = T.rank_of(core)
-    eng2 = 8 // len(served_chips(0))
+    eng2 = 8 // len(GROUPS[0])
+    sp = [r for r in range(NR) if any(sg[2] for sg in segments(offs[r], widths[r], yw))][0]
+    sp_core = T.cores[sp]
+    sp_chip = topo.chip(sp_core)
+    sp_help = 8 * sp_chip + HCORES[1]
 
     if rank is not None:
         g.sync.dma_start(T.xs[:], T.x[:]).then_inc(T.sem.ld, 16)
+        g.sync.dma_start(T.xb[:], T.x[:, offs[sp]:offs[sp] + SPW]).then_inc(T.sem.ld2, 16)
         g.wait_ge(T.sem.ld, 16)
         trs = []
         for j in range(P):
-            hs = [helper_core(j, q) for q in range(G)]
+            hs = [helper_core(j, q, sp_chip) for q in range(G)]
             trs.append(RemoteDMATransfer(
                 dst_ids=[dst_id(topo, h) for h in hs], dma_engine_mask=1 << j, remote_sem=T.sem.arr,
                 srcs=[blk(T.xs, j)], dsts=[blk(T.land, rank) for h in hs], alu_op=0))
         g.remote_dma_fused(trs, local_sem=T.sem.snt)
+        g.wait_ge(T.sem.ld2, 16)
+        a = topo.addr(sp_help)
+        g.remote_dma(blk(T.lb, rank), T.xb[:], T.sem.arr, T.sem.snt, a[1], a[0], 1 << P)
         w = widths[rank]
-        if w > 0:
+        if rank == sp:
+            g.sync.wait_ge(T.sem.res, 16)
+            g.sync.dma_start(T.y[:, 0:SPW], T.sb[:]).then_inc(T.sem.st, 16)
+            g.wait_ge(T.sem.res, 16)
+            g.wait_ge(T.sem.st, 16)
+        elif w > 0:
             need = P * eng2
             hw = [g.sync, g.scalar]
-            waited = [False, False]
-            nhw = 0
-            nsw = 0
-            for c, e, lone in segments(offs[rank], w, T.y.shape[1]):
-                src = T.s[c // NCOL::P, c % NCOL:c % NCOL + e - c]
-                dst = T.y[:, c - offs[rank]:e - offs[rank]]
-                if lone:
-                    g.wait_ge(T.sem.res, need)
-                    g.dma_start(dst, src, allow_slow_non_contiguous=True).then_inc(T.sem.stg, 16)
-                    nsw += 1
-                else:
-                    k = nhw % 2
-                    if not waited[k]:
-                        hw[k].wait_ge(T.sem.res, need)
-                        waited[k] = True
-                    hw[k].dma_start(dst, src).then_inc(T.sem.st, 16)
-                    nhw += 1
+            n = 0
+            for c, e, lone in segments(offs[rank], w, yw):
+                hw[n].wait_ge(T.sem.res, need)
+                hw[n].dma_start(T.y[:, c - offs[rank]:e - offs[rank]],
+                                T.s[c // NCOL::P, c % NCOL:c % NCOL + e - c]).then_inc(T.sem.st, 16)
+                n += 1
             g.wait_ge(T.sem.res, need)
-            if nhw:
-                g.wait_ge(T.sem.st, 16 * nhw)
-            if nsw:
-                g.wait_ge(T.sem.stg, 16 * nsw)
-        g.wait_ge(T.sem.snt, P)
+            g.wait_ge(T.sem.st, 16 * n)
+        g.wait_ge(T.sem.snt, P + 1)
         return
 
+    if core == sp_help:
+        g.wait_ge(T.sem.arr, NR)
+        g.remote_dma_fused([RemoteDMATransfer(
+            dst_ids=[dst_id(topo, sp_core)], dma_engine_mask=0xFFFF, remote_sem=T.sem.res,
+            srcs=[blk(T.lb, i) for i in range(NR)], dsts=[T.sb[:]], alu_op=1)], local_sem=T.sem.snt)
+        g.wait_ge(T.sem.snt, 16)
+        return
     for j in range(P):
         for q in range(G):
-            if helper_core(j, q) != core:
+            if helper_core(j, q, sp_chip) != core:
                 continue
             g.wait_ge(T.sem.arr, NR)
-            srcs = [blk(T.land, i) for i in range(NR)]
             trs = []
-            for t, ch in enumerate(served_chips(q)):
-                ds = [c for c in T.cores if topo.chip(c) == ch and widths[T.rank_of(c)] > 0]
+            for t, ch in enumerate(GROUPS[q]):
+                ds = [c for c in T.cores if topo.chip(c) == ch and widths[T.rank_of(c)] > 0 and c != sp_core]
                 trs.append(RemoteDMATransfer(
                     dst_ids=[dst_id(topo, c) for c in ds],
                     dma_engine_mask=((1 << eng2) - 1) << (eng2 * t), remote_sem=T.sem.res,
-                    srcs=srcs, dsts=[blk(T.s, j) for c in ds], alu_op=1))
+                    srcs=[blk(T.land, i) for i in range(NR)], dsts=[blk(T.s, j) for c in ds], alu_op=1))
             g.remote_dma_fused(trs, local_sem=T.sem.snt)
             g.wait_ge(T.sem.snt, eng2 * len(trs))

@@ -57,7 +57,7 @@ def rank_program(g, core, T, topo):
     offs = T.tables["OFF"]
     yw = 16
     rank = T.rank_of(core)
-    eng2 = 8 // len(GROUPS[0])
+    chip = topo.chip(core)
     sp = [r for r in range(NR) if any(sg[2] for sg in segments(offs[r], widths[r], yw))][0]
     sp_core = T.cores[sp]
     sp_chip = topo.chip(sp_core)
@@ -84,7 +84,7 @@ def rank_program(g, core, T, topo):
             g.wait_ge(T.sem.res, 16)
             g.wait_ge(T.sem.st, 16)
         elif w > 0:
-            need = P * eng2
+            need = 8 * P
             hw = [g.sync, g.scalar]
             n = 0
             for c, e, lone in segments(offs[rank], w, yw):
@@ -109,12 +109,14 @@ def rank_program(g, core, T, topo):
             if helper_core(j, q, sp_chip) != core:
                 continue
             g.wait_ge(T.sem.arr, NR)
+            served = [c for c in T.cores
+                      if topo.chip(c) in GROUPS[q] and widths[T.rank_of(c)] > 0 and c != sp_core]
             trs = []
-            for t, ch in enumerate(GROUPS[q]):
-                ds = [c for c in T.cores if topo.chip(c) == ch and widths[T.rank_of(c)] > 0 and c != sp_core]
-                trs.append(RemoteDMATransfer(
-                    dst_ids=[dst_id(topo, c) for c in ds],
-                    dma_engine_mask=((1 << eng2) - 1) << (eng2 * t), remote_sem=T.sem.res,
-                    srcs=[blk(T.land, i) for i in range(NR)], dsts=[blk(T.s, j) for c in ds], alu_op=1))
+            for mask, ds in ((0x00FF, [c for c in served if topo.chip(c) != chip]),
+                             (0xFF00, [c for c in served if topo.chip(c) == chip])):
+                if ds:
+                    trs.append(RemoteDMATransfer(
+                        dst_ids=[dst_id(topo, c) for c in ds], dma_engine_mask=mask, remote_sem=T.sem.res,
+                        srcs=[blk(T.land, i) for i in range(NR)], dsts=[blk(T.s, j) for c in ds], alu_op=1))
             g.remote_dma_fused(trs, local_sem=T.sem.snt)
-            g.wait_ge(T.sem.snt, eng2 * len(trs))
+            g.wait_ge(T.sem.snt, 8 * len(trs))

@@ -27,6 +27,14 @@ def helper_core(j, q, sp_chip):
     return 8 * rest[j - len(chips)] + HCORES[1]
 
 
+def links(topo, a, b):
+    ca = topo.chip(a)
+    cb = topo.chip(b)
+    if ca == cb:
+        return 0
+    return 1 if topo.mates(ca, cb) or topo.same_plane(ca, cb) else 2
+
+
 def blk(t, k):
     return t[128 * k:128 * (k + 1), :]
 
@@ -69,7 +77,7 @@ def rank_program(g, core, T, topo):
         g.wait_ge(T.sem.ld, 16)
         trs = []
         for j in range(P):
-            hs = [helper_core(j, q, sp_chip) for q in range(G)]
+            hs = sorted([helper_core(j, q, sp_chip) for q in range(G)], key=lambda h: -links(topo, core, h))
             trs.append(RemoteDMATransfer(
                 dst_ids=[dst_id(topo, h) for h in hs], dma_engine_mask=1 << j, remote_sem=T.sem.arr,
                 srcs=[blk(T.xs, j)], dsts=[blk(T.land, rank) for h in hs], alu_op=0))

from concourse.bass import DstId, RemoteDMATransfer

P = 7
NCOL = 12
GROUPS = [[0, 2, 4, 6], [1, 3, 5, 7]]
HCORES = [4, 5]
SPW = 4
G = len(GROUPS)
NR = 16

SCRATCH = {
    "xs": ("dram", [P * 128, NCOL], "bfloat16"),
    "land": ("dram", [NR * 128, NCOL], "bfloat16"),
    "s": ("dram", [P * 128, NCOL], "bfloat16"),
    "xb": ("dram", [128, SPW], "bfloat16"),
    "lb": ("dram", [NR * 128, SPW], "bfloat16"),
    "sb": ("dram", [128, SPW], "bfloat16"),
}
SEMAPHORES = ["ld", "ld2", "snt", "arr", "res", "st"]


def helper_core(j, q, sp_chip):
    chips = GROUPS[q]
    if j < len(chips):
        return 8 * chips[j] + HCORES[0]
    rest = [ch for ch in chips if ch != sp_chip]
    return 8 * rest[j - len(chips)] + HCORES[1]


def links(topo, a, b):
    ca = topo.chip(a)
    cb = topo.chip(b)
    if ca == cb:
        return 0
    return 1 if topo.mates(ca, cb) or topo.same_plane(ca, cb) else 2


def blk(t, k):
    return t[128 * k:128 * (k + 1), :]


def segments(off, w, yw):
    out = []
    c = off
    while c < off + w:
        e = min(off + w, (c // NCOL + 1) * NCOL)
        out.append([c, e, False])
        c = e
    for k, sg in enumerate(out):
        if sg[1] - sg[0] == 1:
            if k == len(out) - 1 and sg[0] % NCOL + 2 <= NCOL and sg[0] - off + 2 <= yw:
                sg[1] += 1
            else:
                sg[2] = True
    return out


def dst_id(topo, c):
    a = topo.addr(c)
    return DstId(rid=a[0], pnc=a[1])


def rank_program(g, core, T, topo):
    widths = T.tables["WIDTHS"]
    offs = T.tables["OFF"]
    yw = 16
    rank = T.rank_of(core)
    chip = topo.chip(core)
    sp = [r for r in range(NR) if any(sg[2] for sg in segments(offs[r], widths[r], yw))][0]
    sp_core = T.cores[sp]
    sp_chip = topo.chip(sp_core)
    sp_help = 8 * sp_chip + HCORES[1]

    if rank is not None:
        g.sync.dma_start(T.xs[:], T.x[:]).then_inc(T.sem.ld, 16)
        g.sync.dma_start(T.xb[:], T.x[:, offs[sp]:offs[sp] + SPW]).then_inc(T.sem.ld2, 16)
        g.wait_ge(T.sem.ld, 16)
        trs = []
        for j in range(P):
            hs = sorted([helper_core(j, q, sp_chip) for q in range(G)], key=lambda h: -links(topo, core, h))
            trs.append(RemoteDMATransfer(
                dst_ids=[dst_id(topo, h) for h in hs], dma_engine_mask=1 << j, remote_sem=T.sem.arr,
                srcs=[blk(T.xs, j)], dsts=[blk(T.land, rank) for h in hs], alu_op=0))
        g.remote_dma_fused(trs, local_sem=T.sem.snt)
        g.wait_ge(T.sem.ld2, 16)
        a = topo.addr(sp_help)
        g.remote_dma(blk(T.lb, rank), T.xb[:], T.sem.arr, T.sem.snt, a[1], a[0], 1 << P)
        w = widths[rank]
        if rank == sp:
            g.sync.wait_ge(T.sem.res, 16)
            g.sync.dma_start(T.y[:, 0:SPW], T.sb[:]).then_inc(T.sem.st, 16)
            g.wait_ge(T.sem.res, 16)
            g.wait_ge(T.sem.st, 16)
        elif w > 0:
            need = 8 * P
            hw = [g.sync, g.scalar]
            n = 0
            for c, e, lone in segments(offs[rank], w, yw):
                hw[n].wait_ge(T.sem.res, need)
                hw[n].dma_start(T.y[:, c - offs[rank]:e - offs[rank]],
                                T.s[c // NCOL::P, c % NCOL:c % NCOL + e - c]).then_inc(T.sem.st, 16)
                n += 1
            g.wait_ge(T.sem.res, need)
            g.wait_ge(T.sem.st, 16 * n)
        g.wait_ge(T.sem.snt, P + 1)
        return

    if core == sp_help:
        g.wait_ge(T.sem.arr, NR)
        g.remote_dma_fused([RemoteDMATransfer(
            dst_ids=[dst_id(topo, sp_core)], dma_engine_mask=0xFFFF, remote_sem=T.sem.res,
            srcs=[blk(T.lb, i) for i in range(NR)], dsts=[T.sb[:]], alu_op=1)], local_sem=T.sem.snt)
        g.wait_ge(T.sem.snt, 16)
        return
    for j in range(P):
        for q in range(G):
            if helper_core(j, q, sp_chip) != core:
                continue
            g.wait_ge(T.sem.arr, NR)
            served = [c for c in T.cores
                      if topo.chip(c) in GROUPS[q] and widths[T.rank_of(c)] > 0 and c != sp_core]
            trs = []
            for mask, ds in ((0x00FF, [c for c in served if topo.chip(c) != chip]),
                             (0xFF00, [c for c in served if topo.chip(c) == chip])):
                if ds:
                    trs.append(RemoteDMATransfer(
                        dst_ids=[dst_id(topo, c) for c in ds], dma_engine_mask=mask, remote_sem=T.sem.res,
                        srcs=[blk(T.land, i) for i in range(NR)], dsts=[blk(T.s, j) for c in ds], alu_op=1))
            g.remote_dma_fused(trs, local_sem=T.sem.snt)
            g.wait_ge(T.sem.snt, 8 * len(trs))
